import numpy as np, ml_dtypes
CORES = [100,101,102,103,108,109,110,111]
N = 8
import mx_ref
NC, GR, GC, T = 512, 4, 2, 4
TA, TB = T // GC, T // GR
BF = ml_dtypes.bfloat16
def setup_inputs(rng):
    def f(*shape):
        return mx_ref.flush((rng.standard_normal(shape, dtype=np.float32) * np.exp2(rng.integers(-2, 3, shape[:-1] + (1,)))).astype(BF))
    return {"a": f(N, 128, TA * 512), "b": f(N, 128, TB * 4 * NC)}
def setup_inputs_blocks(rng):
    d = setup_inputs(rng)
    for k in ("a", "b"): d[k] = mx_ref.spread(d[k], rng, 1)
    return d
def setup_inputs_wide(rng):
    d = setup_inputs(rng)
    for k in ("a", "b"): d[k] = mx_ref.flush((d[k].astype(np.float32) * np.exp2(rng.integers(-8, 9, (N, 1, 1))).astype(np.float32)).astype(BF))
    return d
def setup_inputs_zeros(rng):
    d = setup_inputs(rng); v = d["b"].reshape(N, 128, -1, 4).copy()
    v[np.broadcast_to((rng.random((N, 1, v.shape[2], 1)) < 0.33), v.shape)] = 0
    d["b"] = v.reshape(d["b"].shape)
    return d
def reference(a, b):
    A = lambda i, s: mx_ref.quantize(a[i * GC + s // TA][:, 512 * (s % TA):512 * (s % TA) + 512])
    B = lambda s, j: mx_ref.quantize(b[(s // TB) * GC + j][:, 4 * NC * (s % TB):4 * NC * (s % TB) + 4 * NC])
    y = np.zeros((N, 128, NC), np.float32)
    for r in range(N):
        for s in range(T):
            p = mx_ref.matmul(A(r // GC, s), B(s, r % GC))
            y[r] = p if s == 0 else y[r] + p
    return {"y": y}

@@ -1,0 +1,158 @@
+from concourse.bass import DstId, RemoteDMATransfer
+from concourse.mybir import dt, ActivationFunctionType
+
+GR, GC = 4, 2
+TA = GR // GC
+AW, BW = 128, 512
+HW = BW // 2
+SPARE = False
+
+SCRATCH = {
+    "a_in": ("sbuf", [128, TA * 4 * AW], "bfloat16"),
+    "b_in": ("sbuf", [128, 4 * BW], "bfloat16"),
+    "aq": ("sbuf", [128, GR * AW], "float8_e4m3fn_x4"),
+    "asc": ("sbuf", [128, GR * AW], "uint8"),
+    "bq": ("sbuf", [128, GR * BW], "float8_e4m3fn_x4"),
+    "bsc": ("sbuf", [128, GR * BW], "uint8"),
+    "acc": ("psum", [128, 2 * 512], "float32"),
+    "y_sb": ("sbuf", [128, BW], "float32"),
+}
+SEMAPHORES = (["la", "lb", "qa", "qb", "ra", "sent", "mm0", "mm1", "cp0", "cp1", "st0", "st1"]
+              + ["bs%d" % s for s in range(GR)] + ["bc%d" % s for s in range(GR)])
+
+
+def _bits(mask):
+    return bin(mask).count("1")
+
+
+def _plan(T, topo):
+    plans, leaving = [], {}
+    for j in range(GC):
+        col = [T.cores[s * GC + j] for s in range(GR)]
+        hops = []
+        for s, own in enumerate(col):
+            near = [c for c in col if c != own and topo.chip(c) == topo.chip(own)]
+            far = [c for c in col if topo.chip(c) != topo.chip(own)]
+            entry = ([c for c in far if not topo.may_write(c, own)] + far)[0]
+            if topo.may_write(own, entry):
+                hops.append((0, s, own, entry))
+                landed = 1
+            else:
+                if SPARE:
+                    carrier = [c for c in range(topo.CORES_PER_CHIP * topo.CHIPS)
+                               if topo.chip(c) == topo.chip(own) and T.rank_of(c) is None
+                               and topo.die(c) != topo.die(own) and topo.may_write(c, entry)][j]
+                    hops.append((0, s, own, carrier))
+                else:
+                    carrier = [c for c in near if topo.may_write(c, entry)][0]
+                hops.append((1, s, carrier, entry))
+                landed = 2
+            hops += [(0, s, own, c) for c in near]
+            hops += [(landed, s, entry, c) for c in far if c != entry]
+        for _, _, src, dst in hops:
+            if topo.chip(src) != topo.chip(dst):
+                leaving[src] = topo.mask(src, dst)
+        plans.append(sorted(hops, key=lambda h: h[0]))
+    return plans, leaving
+
+
+def rank_program(g, core, T, topo):
+    rank = T.rank_of(core)
+    sem = T.sem
+    plans, leaving = _plan(T, topo)
+    if rank is None:
+        serves = [jj for jj in range(GC) if any(h[2] == core for h in plans[jj])]
+        if not serves:
+            return
+        i, j = None, serves[0]
+    else:
+        i, j = rank // GC, rank % GC
+    sent = [0]
+
+    def engines(src, dst):
+        mask = topo.mask(src, dst)
+        if topo.chip(src) == topo.chip(dst):
+            mask &= ~leaving.get(src, 0)
+        return mask
+
+    def send(view, targets, remote_sem):
+        if len(targets) == 1:
+            dst, mask = targets[0]
+            rid, pid, _ = topo.addr(dst)
+            g.remote_dma(view(), view(), remote_sem, sem.sent, pid, rid, mask)
+        else:
+            trs = []
+            for dst, mask in targets:
+                rid, pid, _ = topo.addr(dst)
+                trs.append(RemoteDMATransfer(dst_ids=[DstId(rid=rid, pnc=pid)], dma_engine_mask=mask,
+                                             remote_sem=remote_sem, src=view(), dst=view()))
+            g.remote_dma_fused(trs, local_sem=sem.sent)
+        sent[0] += sum(_bits(m) for _, m in targets)
+
+    row = [] if rank is None else [T.cores[i * GC + jj] for jj in range(GC) if jj != j]
+    if rank is not None:
+        a0, b0 = TA * AW * j, BW * i
+        g.sync.dma_start(T.a_in[:], T.a[:]).then_inc(sem.la, 16)
+        g.sync.dma_start(T.b_in[:], T.b[:]).then_inc(sem.lb, 16)
+        g.vector.wait_ge(sem.la, 16)
+        g.vector.quantize_mx(T.aq[:, a0:a0 + TA * AW], T.asc[:, a0:a0 + TA * AW], T.a_in[:]).then_inc(sem.qa, 1)
+        g.vector.wait_ge(sem.lb, 16)
+        g.vector.quantize_mx(T.bq[:, b0:b0 + BW], T.bsc[:, b0:b0 + BW], T.b_in[:]).then_inc(sem.qb, 1)
+        g.wait_ge(sem.qa, 1)
+        for peer in row:
+            send(lambda: T.asc[:, a0:a0 + TA * AW], [(peer, topo.mask(core, peer))], sem.ra)
+
+    lands = {s: (stage, _bits(engines(src, dst))) for stage, s, src, dst in plans[j] if dst == core}
+    calls = []
+    for _, s, src, dst in plans[j]:
+        if src == core:
+            mask = engines(src, dst)
+            if calls and calls[-1][0] == s and not any(mask & m for _, m in calls[-1][1]):
+                calls[-1][1].append((dst, mask))
+            else:
+                calls.append((s, [(dst, mask)]))
+    a_codes_due = rank is not None
+    for s, targets in calls:
+        c0 = BW * s
+        if s != i and a_codes_due:
+            a_codes_due = False
+            for peer in row:
+                send(lambda: T.aq[:, a0:a0 + TA * AW].bitcast(dt.uint8), [(peer, engines(core, peer))], sem.ra)
+        g.wait_ge(sem.qb, 1) if s == i else g.wait_ge(sem["bs%d" % s], lands[s][1])
+        send(lambda: T.bsc[:, c0:c0 + BW], targets, sem["bs%d" % s])
+        if s != i:
+            g.wait_ge(sem["bc%d" % s], lands[s][1])
+        send(lambda: T.bq[:, c0:c0 + BW].bitcast(dt.uint8), targets, sem["bc%d" % s])
+    if a_codes_due:
+        for peer in row:
+            send(lambda: T.aq[:, a0:a0 + TA * AW].bitcast(dt.uint8), [(peer, engines(core, peer))], sem.ra)
+    g.wait_ge(sem.sent, sent[0])
+    if rank is None:
+        return
+
+    order = sorted(range(GR), key=lambda s: (-1, 0) if s == i else (lands[s][0], s))
+    g.tensor.wait_ge(sem.qa, 1)
+    g.tensor.wait_ge(sem.ra, sum(_bits(topo.mask(peer, core)) + _bits(engines(peer, core)) for peer in row))
+    for k, s in enumerate(order):
+        if s == i:
+            g.tensor.wait_ge(sem.qb, 1)
+        else:
+            g.tensor.wait_ge(sem["bs%d" % s], lands[s][1])
+            g.tensor.wait_ge(sem["bc%d" % s], lands[s][1])
+        for h in range(2):
+            c0 = BW * s + HW * h
+            g.tensor.matmul_mx(T.acc[:, 512 * h:512 * h + HW],
+                               T.aq[:, AW * s:AW * s + AW], T.asc[:, AW * s:AW * s + AW],
+                               T.bq[:, c0:c0 + HW], T.bsc[:, c0:c0 + HW],
+                               k == 0, k == GR - 1).then_inc(sem["mm%d" % h], 1)
+
+    g.vector.wait_ge(sem.mm0, GR)
+    g.vector.tensor_copy(T.y_sb[:, 0:HW], T.acc[:, 0:HW]).then_inc(sem.cp0, 1)
+    g.sync.wait_ge(sem.cp0, 1)
+    g.sync.dma_start(T.y[:, 0:HW], T.y_sb[:, 0:HW]).then_inc(sem.st0, 16)
+    g.sync.wait_ge(sem.st0, 16)
+    g.scalar.wait_ge(sem.mm1, GR)
+    g.scalar.activation(T.y_sb[:, HW:BW], T.acc[:, 512:512 + HW], ActivationFunctionType.Copy).then_inc(sem.cp1, 1)
+    g.scalar.wait_ge(sem.cp1, 1)
+    g.scalar.dma_start(T.y[:, HW:BW], T.y_sb[:, HW:BW]).then_inc(sem.st1, 16)
+    g.scalar.wait_ge(sem.st1, 16)

@@ -5,7 +5,6 @@ GR, GC = 4, 2
 TA = GR // GC
 AW, BW = 128, 512
 HW = BW // 2
-SPARE = False
 
 SCRATCH = {
     "a_in": ("sbuf", [128, TA * 4 * AW], "bfloat16"),
@@ -34,21 +33,18 @@ def _plan(T, topo):
             near = [c for c in col if c != own and topo.chip(c) == topo.chip(own)]
             far = [c for c in col if topo.chip(c) != topo.chip(own)]
             entry = ([c for c in far if not topo.may_write(c, own)] + far)[0]
+            rest = [c for c in far if c != entry]
             if topo.may_write(own, entry):
                 hops.append((0, s, own, entry))
-                landed = 1
+                hops += [(1, s, entry, c) for c in rest]
             else:
-                if SPARE:
-                    carrier = [c for c in range(topo.CORES_PER_CHIP * topo.CHIPS)
-                               if topo.chip(c) == topo.chip(own) and T.rank_of(c) is None
-                               and topo.die(c) != topo.die(own) and topo.may_write(c, entry)][j]
-                    hops.append((0, s, own, carrier))
-                else:
-                    carrier = [c for c in near if topo.may_write(c, entry)][0]
-                hops.append((1, s, carrier, entry))
-                landed = 2
+                spare = [c for c in range(topo.CORES_PER_CHIP * topo.CHIPS)
+                         if topo.chip(c) == topo.chip(own) and T.rank_of(c) is None
+                         and topo.die(c) != topo.die(own) and topo.may_write(c, entry)][j]
+                door = (rest + [entry])[0]
+                hops += [(0, s, own, spare), (1, s, spare, door)]
+                hops += [(2, s, door, c) for c in far if c != door]
             hops += [(0, s, own, c) for c in near]
-            hops += [(landed, s, entry, c) for c in far if c != entry]
         for _, _, src, dst in hops:
             if topo.chip(src) != topo.chip(dst):
                 leaving[src] = topo.mask(src, dst)
@@ -69,9 +65,9 @@ def rank_program(g, core, T, topo):
         i, j = rank // GC, rank % GC
     sent = [0]
 
-    def engines(src, dst):
+    def engines(src, dst, relay=False):
         mask = topo.mask(src, dst)
-        if topo.chip(src) == topo.chip(dst):
+        if topo.chip(src) == topo.chip(dst) and not relay:
             mask &= ~leaving.get(src, 0)
         return mask
 
@@ -102,11 +98,11 @@ def rank_program(g, core, T, topo):
         for peer in row:
             send(lambda: T.asc[:, a0:a0 + TA * AW], [(peer, topo.mask(core, peer))], sem.ra)
 
-    lands = {s: (stage, _bits(engines(src, dst))) for stage, s, src, dst in plans[j] if dst == core}
+    lands = {s: (stage, _bits(engines(src, dst, stage > 0))) for stage, s, src, dst in plans[j] if dst == core}
     calls = []
-    for _, s, src, dst in plans[j]:
+    for stage, s, src, dst in plans[j]:
         if src == core:
-            mask = engines(src, dst)
+            mask = engines(src, dst, stage > 0)
             if calls and calls[-1][0] == s and not any(mask & m for _, m in calls[-1][1]):
                 calls[-1][1].append((dst, mask))
             else:
@@ -123,14 +119,12 @@ def rank_program(g, core, T, topo):
         if s != i:
             g.wait_ge(sem["bc%d" % s], lands[s][1])
         send(lambda: T.bq[:, c0:c0 + BW].bitcast(dt.uint8), targets, sem["bc%d" % s])
-    if a_codes_due:
-        for peer in row:
-            send(lambda: T.aq[:, a0:a0 + TA * AW].bitcast(dt.uint8), [(peer, engines(core, peer))], sem.ra)
     g.wait_ge(sem.sent, sent[0])
     if rank is None:
         return
 
-    order = sorted(range(GR), key=lambda s: (-1, 0) if s == i else (lands[s][0], s))
+    order = sorted(range(GR), key=lambda s: (-1, 0) if s == i
+                   else (lands[s][0], not topo.may_write(T.cores[s * GC + j], core)))
     g.tensor.wait_ge(sem.qa, 1)
     g.tensor.wait_ge(sem.ra, sum(_bits(topo.mask(peer, core)) + _bits(engines(peer, core)) for peer in row))
     for k, s in enumerate(order):

@@ -4,7 +4,8 @@ from concourse.mybir import dt, ActivationFunctionType
 GR, GC = 4, 2
 TA = GR // GC
 AW, BW = 128, 512
-HW = BW // 2
+CUT = 384
+GROUPS = [(0, 192), (192, CUT), (CUT, BW)]
 
 SCRATCH = {
     "a_in": ("sbuf", [128, TA * 4 * AW], "bfloat16"),
@@ -13,11 +14,12 @@ SCRATCH = {
     "asc": ("sbuf", [128, GR * AW], "uint8"),
     "bq": ("sbuf", [128, GR * BW], "float8_e4m3fn_x4"),
     "bsc": ("sbuf", [128, GR * BW], "uint8"),
-    "acc": ("psum", [128, 2 * 512], "float32"),
+    "acc": ("psum", [128, len(GROUPS) * 512], "float32"),
     "y_sb": ("sbuf", [128, BW], "float32"),
 }
-SEMAPHORES = (["la", "lb", "qa", "qb", "ra", "sent", "mm0", "mm1", "cp0", "cp1", "st0", "st1"]
-              + ["bs%d" % s for s in range(GR)] + ["bc%d" % s for s in range(GR)])
+SEMAPHORES = (["la", "lb", "qa", "qb", "ra", "sent"]
+              + [n + "%d" % k for n in ("mm", "cp", "st") for k in range(len(GROUPS))]
+              + ["b" + part + "%d" % s for part in "scd" for s in range(GR)])
 
 
 def _bits(mask):
@@ -28,27 +30,31 @@ def _plan(T, topo):
     plans, leaving = [], {}
     for j in range(GC):
         col = [T.cores[s * GC + j] for s in range(GR)]
-        hops = []
+        hops, cut = [], set()
         for s, own in enumerate(col):
             near = [c for c in col if c != own and topo.chip(c) == topo.chip(own)]
             far = [c for c in col if topo.chip(c) != topo.chip(own)]
             entry = ([c for c in far if not topo.may_write(c, own)] + far)[0]
-            rest = [c for c in far if c != entry]
             if topo.may_write(own, entry):
-                hops.append((0, s, own, entry))
-                hops += [(1, s, entry, c) for c in rest]
+                for part in "sc":
+                    hops += [(0, s, part, own, c) for c in [entry] + near]
+                    hops += [(1, s, part, entry, c) for c in far if c != entry]
             else:
+                cut.add(s)
+                mate = [c for c in near if topo.may_write(c, entry)][0]
                 spare = [c for c in range(topo.CORES_PER_CHIP * topo.CHIPS)
                          if topo.chip(c) == topo.chip(own) and T.rank_of(c) is None
                          and topo.die(c) != topo.die(own) and topo.may_write(c, entry)][j]
-                door = (rest + [entry])[0]
-                hops += [(0, s, own, spare), (1, s, spare, door)]
-                hops += [(2, s, door, c) for c in far if c != door]
-            hops += [(0, s, own, c) for c in near]
-        for _, _, src, dst in hops:
+                door = ([c for c in far if c != entry] + [entry])[0]
+                hops += [(0, s, "s", own, spare), (0, s, "c", own, spare), (0, s, "d", own, mate)]
+                hops += [(0, s, part, own, c) for c in near for part in "scd" if (part, c) != ("d", mate)]
+                hops += [(1, s, "s", spare, door), (1, s, "c", spare, door), (1, s, "d", mate, entry)]
+                hops += [(2, s, part, door, c) for part in "sc" for c in far if c != door]
+                hops += [(2, s, "d", entry, c) for c in far if c != entry]
+        for _, _, _, src, dst in hops:
             if topo.chip(src) != topo.chip(dst):
                 leaving[src] = topo.mask(src, dst)
-        plans.append(sorted(hops, key=lambda h: h[0]))
+        plans.append((sorted(hops, key=lambda h: h[0]), cut))
     return plans, leaving
 
 
@@ -57,19 +63,26 @@ def rank_program(g, core, T, topo):
     sem = T.sem
     plans, leaving = _plan(T, topo)
     if rank is None:
-        serves = [jj for jj in range(GC) if any(h[2] == core for h in plans[jj])]
+        serves = [jj for jj in range(GC) if any(h[3] == core for h in plans[jj][0])]
         if not serves:
             return
         i, j = None, serves[0]
     else:
         i, j = rank // GC, rank % GC
+    hops, cut = plans[j]
     sent = [0]
 
-    def engines(src, dst, relay=False):
+    def engines(src, dst, late=False):
         mask = topo.mask(src, dst)
-        if topo.chip(src) == topo.chip(dst) and not relay:
+        if topo.chip(src) == topo.chip(dst) and not late:
             mask &= ~leaving.get(src, 0)
         return mask
+
+    def piece(s, part):
+        lo, hi = (0, BW) if part == "s" or s not in cut else (0, CUT) if part == "c" else (CUT, BW)
+        if part == "s":
+            return lambda: T.bsc[:, BW * s + lo:BW * s + hi]
+        return lambda: T.bq[:, BW * s + lo:BW * s + hi].bitcast(dt.uint8)
 
     def send(view, targets, remote_sem):
         if len(targets) == 1:
@@ -97,56 +110,67 @@ def rank_program(g, core, T, topo):
         g.wait_ge(sem.qa, 1)
         for peer in row:
             send(lambda: T.asc[:, a0:a0 + TA * AW], [(peer, topo.mask(core, peer))], sem.ra)
+        g.wait_ge(sem.qb, 1)
 
-    lands = {s: (stage, _bits(engines(src, dst, stage > 0))) for stage, s, src, dst in plans[j] if dst == core}
-    calls = []
-    for stage, s, src, dst in plans[j]:
+    lands, calls = {}, []
+    for stage, s, part, src, dst in hops:
+        mask = engines(src, dst, stage > 0 and part != "s")
+        if dst == core:
+            lands[s, part] = (stage, topo.chip(src) == topo.chip(core), _bits(mask))
         if src == core:
-            mask = engines(src, dst, stage > 0)
-            if calls and calls[-1][0] == s and not any(mask & m for _, m in calls[-1][1]):
-                calls[-1][1].append((dst, mask))
+            if calls and calls[-1][:2] == (s, part) and not any(mask & m for _, m in calls[-1][2]):
+                calls[-1][2].append((dst, mask))
             else:
-                calls.append((s, [(dst, mask)]))
+                calls.append((s, part, [(dst, mask)]))
     a_codes_due = rank is not None
-    for s, targets in calls:
-        c0 = BW * s
-        if s != i and a_codes_due:
-            a_codes_due = False
-            for peer in row:
-                send(lambda: T.aq[:, a0:a0 + TA * AW].bitcast(dt.uint8), [(peer, engines(core, peer))], sem.ra)
-        g.wait_ge(sem.qb, 1) if s == i else g.wait_ge(sem["bs%d" % s], lands[s][1])
-        send(lambda: T.bsc[:, c0:c0 + BW], targets, sem["bs%d" % s])
+    for s, part, targets in calls:
         if s != i:
-            g.wait_ge(sem["bc%d" % s], lands[s][1])
-        send(lambda: T.bq[:, c0:c0 + BW].bitcast(dt.uint8), targets, sem["bc%d" % s])
+            if a_codes_due:
+                a_codes_due = False
+                for peer in row:
+                    send(lambda: T.aq[:, a0:a0 + TA * AW].bitcast(dt.uint8), [(peer, engines(core, peer))], sem.ra)
+            g.wait_ge(sem["b%s%d" % (part, s)], lands[s, part][2])
+        send(piece(s, part), targets, sem["b%s%d" % (part, s)])
     g.wait_ge(sem.sent, sent[0])
     if rank is None:
         return
 
-    order = sorted(range(GR), key=lambda s: (-1, 0) if s == i
-                   else (lands[s][0], not topo.may_write(T.cores[s * GC + j], core)))
+    def codes(s, k):
+        return "d" if s in cut and GROUPS[k][0] >= CUT else "c"
+    todo = sorted(((s, k) for s in range(GR) for k in range(len(GROUPS))),
+                  key=lambda e: (-1, 0) if e[0] == i else lands[e[0], codes(*e)][:2])
     g.tensor.wait_ge(sem.qa, 1)
     g.tensor.wait_ge(sem.ra, sum(_bits(topo.mask(peer, core)) + _bits(engines(peer, core)) for peer in row))
-    for k, s in enumerate(order):
-        if s == i:
-            g.tensor.wait_ge(sem.qb, 1)
-        else:
-            g.tensor.wait_ge(sem["bs%d" % s], lands[s][1])
-            g.tensor.wait_ge(sem["bc%d" % s], lands[s][1])
-        for h in range(2):
-            c0 = BW * s + HW * h
-            g.tensor.matmul_mx(T.acc[:, 512 * h:512 * h + HW],
-                               T.aq[:, AW * s:AW * s + AW], T.asc[:, AW * s:AW * s + AW],
-                               T.bq[:, c0:c0 + HW], T.bsc[:, c0:c0 + HW],
-                               k == 0, k == GR - 1).then_inc(sem["mm%d" % h], 1)
+    g.tensor.wait_ge(sem.qb, 1)
+    seen, done = set(), [0] * len(GROUPS)
+    finish = []
+    for s, k in todo:
+        for part in ("s", codes(s, k)):
+            if s != i and (s, part) not in seen:
+                seen.add((s, part))
+                g.tensor.wait_ge(sem["b%s%d" % (part, s)], lands[s, part][2])
+        done[k] += 1
+        lo, hi = BW * s + GROUPS[k][0], BW * s + GROUPS[k][1]
+        g.tensor.matmul_mx(T.acc[:, 512 * k:512 * k + hi - lo],
+                           T.aq[:, AW * s:AW * s + AW], T.asc[:, AW * s:AW * s + AW],
+                           T.bq[:, lo:hi], T.bsc[:, lo:hi],
+                           done[k] == 1, done[k] == GR).then_inc(sem["mm%d" % k], 1)
+        if done[k] == GR:
+            finish.append(k)
 
-    g.vector.wait_ge(sem.mm0, GR)
-    g.vector.tensor_copy(T.y_sb[:, 0:HW], T.acc[:, 0:HW]).then_inc(sem.cp0, 1)
-    g.sync.wait_ge(sem.cp0, 1)
-    g.sync.dma_start(T.y[:, 0:HW], T.y_sb[:, 0:HW]).then_inc(sem.st0, 16)
-    g.sync.wait_ge(sem.st0, 16)
-    g.scalar.wait_ge(sem.mm1, GR)
-    g.scalar.activation(T.y_sb[:, HW:BW], T.acc[:, 512:512 + HW], ActivationFunctionType.Copy).then_inc(sem.cp1, 1)
-    g.scalar.wait_ge(sem.cp1, 1)
-    g.scalar.dma_start(T.y[:, HW:BW], T.y_sb[:, HW:BW]).then_inc(sem.st1, 16)
-    g.scalar.wait_ge(sem.st1, 16)
+    for n, k in enumerate(finish):
+        lo, hi = GROUPS[k]
+        mm, cp, st = sem["mm%d" % k], sem["cp%d" % k], sem["st%d" % k]
+        if n % 2 == 0:
+            g.vector.wait_ge(mm, GR)
+            g.vector.tensor_copy(T.y_sb[:, lo:hi], T.acc[:, 512 * k:512 * k + hi - lo]).then_inc(cp, 1)
+            q = g.sync
+        else:
+            g.scalar.wait_ge(mm, GR)
+            g.scalar.activation(T.y_sb[:, lo:hi], T.acc[:, 512 * k:512 * k + hi - lo],
+                                ActivationFunctionType.Copy).then_inc(cp, 1)
+            q = g.scalar
+        q.wait_ge(cp, 1)
+        q.dma_start(T.y[:, lo:hi], T.y_sb[:, lo:hi]).then_inc(st, 16)
+    for n, k in enumerate(finish):
+        (g.sync if n % 2 == 0 else g.scalar).wait_ge(sem["st%d" % k], 16)

@@ -4,8 +4,8 @@ from concourse.mybir import dt, ActivationFunctionType
 GR, GC = 4, 2
 TA = GR // GC
 AW, BW = 128, 512
-CUT = 384
-GROUPS = [(0, 192), (192, CUT), (CUT, BW)]
+MID, CUT = 192, 384
+GROUPS = [(0, MID), (MID, CUT), (CUT, BW)]
 
 SCRATCH = {
     "a_in": ("sbuf", [128, TA * 4 * AW], "bfloat16"),
@@ -17,9 +17,9 @@ SCRATCH = {
     "acc": ("psum", [128, len(GROUPS) * 512], "float32"),
     "y_sb": ("sbuf", [128, BW], "float32"),
 }
-SEMAPHORES = (["la", "lb", "qa", "qb", "ra", "sent"]
+SEMAPHORES = (["ld", "lb", "la", "qd", "qb", "qa", "ra", "sent"]
               + [n + "%d" % k for n in ("mm", "cp", "st") for k in range(len(GROUPS))]
-              + ["b" + part + "%d" % s for part in "scd" for s in range(GR)])
+              + ["b" + part + "%d" % s for part in "sced" for s in range(GR)])
 
 
 def _bits(mask):
@@ -30,31 +30,31 @@ def _plan(T, topo):
     plans, leaving = [], {}
     for j in range(GC):
         col = [T.cores[s * GC + j] for s in range(GR)]
-        hops, cut = [], set()
+        hops, carried = [], set()
         for s, own in enumerate(col):
             near = [c for c in col if c != own and topo.chip(c) == topo.chip(own)]
             far = [c for c in col if topo.chip(c) != topo.chip(own)]
             entry = ([c for c in far if not topo.may_write(c, own)] + far)[0]
             if topo.may_write(own, entry):
-                for part in "sc":
+                for part in "dsc":
                     hops += [(0, s, part, own, c) for c in [entry] + near]
                     hops += [(1, s, part, entry, c) for c in far if c != entry]
             else:
-                cut.add(s)
+                carried.add(s)
                 mate = [c for c in near if topo.may_write(c, entry)][0]
                 spare = [c for c in range(topo.CORES_PER_CHIP * topo.CHIPS)
                          if topo.chip(c) == topo.chip(own) and T.rank_of(c) is None
                          and topo.die(c) != topo.die(own) and topo.may_write(c, entry)][j]
                 door = ([c for c in far if c != entry] + [entry])[0]
-                hops += [(0, s, "s", own, spare), (0, s, "c", own, spare), (0, s, "d", own, mate)]
-                hops += [(0, s, part, own, c) for c in near for part in "scd" if (part, c) != ("d", mate)]
-                hops += [(1, s, "s", spare, door), (1, s, "c", spare, door), (1, s, "d", mate, entry)]
-                hops += [(2, s, part, door, c) for part in "sc" for c in far if c != door]
+                hops += [(0, s, "d", own, mate)] + [(0, s, part, own, spare) for part in "sce"]
+                hops += [(0.5, s, part, own, c) for c in near for part in "dsce" if (part, c) != ("d", mate)]
+                hops += [(1, s, part, spare, door) for part in "sce"] + [(1, s, "d", mate, entry)]
+                hops += [(2, s, part, door, c) for part in "sce" for c in far if c != door]
                 hops += [(2, s, "d", entry, c) for c in far if c != entry]
         for _, _, _, src, dst in hops:
             if topo.chip(src) != topo.chip(dst):
                 leaving[src] = topo.mask(src, dst)
-        plans.append((sorted(hops, key=lambda h: h[0]), cut))
+        plans.append((sorted(hops, key=lambda h: h[0]), carried))
     return plans, leaving
 
 
@@ -69,7 +69,7 @@ def rank_program(g, core, T, topo):
         i, j = None, serves[0]
     else:
         i, j = rank // GC, rank % GC
-    hops, cut = plans[j]
+    hops, carried = plans[j]
     sent = [0]
 
     def engines(src, dst, late=False):
@@ -79,9 +79,9 @@ def rank_program(g, core, T, topo):
         return mask
 
     def piece(s, part):
-        lo, hi = (0, BW) if part == "s" or s not in cut else (0, CUT) if part == "c" else (CUT, BW)
         if part == "s":
-            return lambda: T.bsc[:, BW * s + lo:BW * s + hi]
+            return lambda: T.bsc[:, BW * s:BW * s + BW]
+        lo, hi = {"c": (0, MID if s in carried else CUT), "e": (MID, CUT), "d": (CUT, BW)}[part]
         return lambda: T.bq[:, BW * s + lo:BW * s + hi].bitcast(dt.uint8)
 
     def send(view, targets, remote_sem):
@@ -101,54 +101,63 @@ def rank_program(g, core, T, topo):
     row = [] if rank is None else [T.cores[i * GC + jj] for jj in range(GC) if jj != j]
     if rank is not None:
         a0, b0 = TA * AW * j, BW * i
+        g.sync.dma_start(T.b_in[:, 4 * CUT:4 * BW], T.b[:, 4 * CUT:4 * BW]).then_inc(sem.ld, 16)
+        g.sync.dma_start(T.b_in[:, 0:4 * CUT], T.b[:, 0:4 * CUT]).then_inc(sem.lb, 16)
         g.sync.dma_start(T.a_in[:], T.a[:]).then_inc(sem.la, 16)
-        g.sync.dma_start(T.b_in[:], T.b[:]).then_inc(sem.lb, 16)
+        g.vector.wait_ge(sem.ld, 16)
+        g.vector.quantize_mx(T.bq[:, b0 + CUT:b0 + BW], T.bsc[:, b0 + CUT:b0 + BW],
+                             T.b_in[:, 4 * CUT:4 * BW]).then_inc(sem.qd, 1)
+        g.vector.wait_ge(sem.lb, 16)
+        g.vector.quantize_mx(T.bq[:, b0:b0 + CUT], T.bsc[:, b0:b0 + CUT], T.b_in[:, 0:4 * CUT]).then_inc(sem.qb, 1)
         g.vector.wait_ge(sem.la, 16)
         g.vector.quantize_mx(T.aq[:, a0:a0 + TA * AW], T.asc[:, a0:a0 + TA * AW], T.a_in[:]).then_inc(sem.qa, 1)
-        g.vector.wait_ge(sem.lb, 16)
-        g.vector.quantize_mx(T.bq[:, b0:b0 + BW], T.bsc[:, b0:b0 + BW], T.b_in[:]).then_inc(sem.qb, 1)
-        g.wait_ge(sem.qa, 1)
-        for peer in row:
-            send(lambda: T.asc[:, a0:a0 + TA * AW], [(peer, topo.mask(core, peer))], sem.ra)
-        g.wait_ge(sem.qb, 1)
 
     lands, calls = {}, []
     for stage, s, part, src, dst in hops:
-        mask = engines(src, dst, stage > 0 and part != "s")
+        mask = engines(src, dst, stage >= 1 and part == ("e" if s in carried else "c"))
         if dst == core:
-            lands[s, part] = (stage, topo.chip(src) == topo.chip(core), _bits(mask))
+            lands[s, part] = (stage, (topo.chip(src) == topo.chip(core)) == (stage >= 1), _bits(mask))
         if src == core:
-            if calls and calls[-1][:2] == (s, part) and not any(mask & m for _, m in calls[-1][2]):
-                calls[-1][2].append((dst, mask))
+            if calls and calls[-1][:3] == (stage, s, part) and not any(mask & m for _, m in calls[-1][3]):
+                calls[-1][3].append((dst, mask))
             else:
-                calls.append((s, part, [(dst, mask)]))
-    a_codes_due = rank is not None
-    for s, part, targets in calls:
+                calls.append((stage, s, part, [(dst, mask)]))
+    a_due = rank is not None
+    waited = set()
+    for stage, s, part, targets in calls:
+        if stage > 0 and a_due:
+            a_due = False
+            g.wait_ge(sem.qa, 1)
+            for peer in row:
+                send(lambda: T.asc[:, a0:a0 + TA * AW], [(peer, engines(core, peer))], sem.ra)
+                send(lambda: T.aq[:, a0:a0 + TA * AW].bitcast(dt.uint8), [(peer, engines(core, peer))], sem.ra)
         if s != i:
-            if a_codes_due:
-                a_codes_due = False
-                for peer in row:
-                    send(lambda: T.aq[:, a0:a0 + TA * AW].bitcast(dt.uint8), [(peer, engines(core, peer))], sem.ra)
             g.wait_ge(sem["b%s%d" % (part, s)], lands[s, part][2])
+        else:
+            for q in ("qd",) if part == "d" else ("qd", "qb") if part == "s" else ("qb",):
+                if q not in waited:
+                    waited.add(q)
+                    g.wait_ge(sem[q], 1)
         send(piece(s, part), targets, sem["b%s%d" % (part, s)])
     g.wait_ge(sem.sent, sent[0])
     if rank is None:
         return
 
     def codes(s, k):
-        return "d" if s in cut and GROUPS[k][0] >= CUT else "c"
+        return "d" if GROUPS[k][0] >= CUT else "e" if s in carried and GROUPS[k][0] >= MID else "c"
     todo = sorted(((s, k) for s in range(GR) for k in range(len(GROUPS))),
                   key=lambda e: (-1, 0) if e[0] == i else lands[e[0], codes(*e)][:2])
-    g.tensor.wait_ge(sem.qa, 1)
-    g.tensor.wait_ge(sem.ra, sum(_bits(topo.mask(peer, core)) + _bits(engines(peer, core)) for peer in row))
-    g.tensor.wait_ge(sem.qb, 1)
-    seen, done = set(), [0] * len(GROUPS)
-    finish = []
+    seen, done, finish = set(), [0] * len(GROUPS), []
     for s, k in todo:
-        for part in ("s", codes(s, k)):
-            if s != i and (s, part) not in seen:
-                seen.add((s, part))
-                g.tensor.wait_ge(sem["b%s%d" % (part, s)], lands[s, part][2])
+        needs = [("qa", 1) if s // TA == j else ("ra", sum(2 * _bits(engines(peer, core)) for peer in row))]
+        if s == i:
+            needs += [("qd", 1), ("qb", 1)]
+        else:
+            needs += [("b%s%d" % (part, s), lands[s, part][2]) for part in ("s", codes(s, k))]
+        for name, count in needs:
+            if name not in seen:
+                seen.add(name)
+                g.tensor.wait_ge(sem[name], count)
         done[k] += 1
         lo, hi = BW * s + GROUPS[k][0], BW * s + GROUPS[k][1]
         g.tensor.matmul_mx(T.acc[:, 512 * k:512 * k + hi - lo],

from concourse.bass import DstId, RemoteDMATransfer
from concourse.mybir import dt, ActivationFunctionType

GR, GC = 4, 2
TA = GR // GC
AW, BW = 128, 512
MID, CUT = 192, 384
GROUPS = [(0, MID), (MID, CUT), (CUT, BW)]

SCRATCH = {
    "a_in": ("sbuf", [128, TA * 4 * AW], "bfloat16"),
    "b_in": ("sbuf", [128, 4 * BW], "bfloat16"),
    "aq": ("sbuf", [128, GR * AW], "float8_e4m3fn_x4"),
    "asc": ("sbuf", [128, GR * AW], "uint8"),
    "bq": ("sbuf", [128, GR * BW], "float8_e4m3fn_x4"),
    "bsc": ("sbuf", [128, GR * BW], "uint8"),
    "acc": ("psum", [128, len(GROUPS) * 512], "float32"),
    "y_sb": ("sbuf", [128, BW], "float32"),
}
SEMAPHORES = (["ld", "lb", "la", "qd", "qb", "qa", "ra", "sent"]
              + [n + "%d" % k for n in ("mm", "cp", "st") for k in range(len(GROUPS))]
              + ["b" + part + "%d" % s for part in "sced" for s in range(GR)])


def _bits(mask):
    return bin(mask).count("1")


def _plan(T, topo):
    plans, leaving = [], {}
    for j in range(GC):
        col = [T.cores[s * GC + j] for s in range(GR)]
        hops, carried = [], set()
        for s, own in enumerate(col):
            near = [c for c in col if c != own and topo.chip(c) == topo.chip(own)]
            far = [c for c in col if topo.chip(c) != topo.chip(own)]
            entry = ([c for c in far if not topo.may_write(c, own)] + far)[0]
            if topo.may_write(own, entry):
                for part in "dsc":
                    hops += [(0, s, part, own, c) for c in [entry] + near]
                    hops += [(1, s, part, entry, c) for c in far if c != entry]
            else:
                carried.add(s)
                mate = [c for c in near if topo.may_write(c, entry)][0]
                spare = [c for c in range(topo.CORES_PER_CHIP * topo.CHIPS)
                         if topo.chip(c) == topo.chip(own) and T.rank_of(c) is None
                         and topo.die(c) != topo.die(own) and topo.may_write(c, entry)][j]
                door = ([c for c in far if c != entry] + [entry])[0]
                hops += [(0, s, "d", own, mate)] + [(0, s, part, own, spare) for part in "sce"]
                hops += [(0.5, s, part, own, c) for c in near for part in "dsce" if (part, c) != ("d", mate)]
                hops += [(1, s, part, spare, door) for part in "sce"] + [(1, s, "d", mate, entry)]
                hops += [(2, s, part, door, c) for part in "sce" for c in far if c != door]
                hops += [(2, s, "d", entry, c) for c in far if c != entry]
        for _, _, _, src, dst in hops:
            if topo.chip(src) != topo.chip(dst):
                leaving[src] = topo.mask(src, dst)
        plans.append((sorted(hops, key=lambda h: h[0]), carried))
    return plans, leaving


def rank_program(g, core, T, topo):
    rank = T.rank_of(core)
    sem = T.sem
    plans, leaving = _plan(T, topo)
    if rank is None:
        serves = [jj for jj in range(GC) if any(h[3] == core for h in plans[jj][0])]
        if not serves:
            return
        i, j = None, serves[0]
    else:
        i, j = rank // GC, rank % GC
    hops, carried = plans[j]
    sent = [0]

    def engines(src, dst, late=False):
        mask = topo.mask(src, dst)
        if topo.chip(src) == topo.chip(dst) and not late:
            mask &= ~leaving.get(src, 0)
        return mask

    def piece(s, part):
        if part == "s":
            return lambda: T.bsc[:, BW * s:BW * s + BW]
        lo, hi = {"c": (0, MID if s in carried else CUT), "e": (MID, CUT), "d": (CUT, BW)}[part]
        return lambda: T.bq[:, BW * s + lo:BW * s + hi].bitcast(dt.uint8)

    def send(view, targets, remote_sem):
        if len(targets) == 1:
            dst, mask = targets[0]
            rid, pid, _ = topo.addr(dst)
            g.remote_dma(view(), view(), remote_sem, sem.sent, pid, rid, mask)
        else:
            trs = []
            for dst, mask in targets:
                rid, pid, _ = topo.addr(dst)
                trs.append(RemoteDMATransfer(dst_ids=[DstId(rid=rid, pnc=pid)], dma_engine_mask=mask,
                                             remote_sem=remote_sem, src=view(), dst=view()))
            g.remote_dma_fused(trs, local_sem=sem.sent)
        sent[0] += sum(_bits(m) for _, m in targets)

    row = [] if rank is None else [T.cores[i * GC + jj] for jj in range(GC) if jj != j]
    if rank is not None:
        a0, b0 = TA * AW * j, BW * i
        g.sync.dma_start(T.b_in[:, 4 * CUT:4 * BW], T.b[:, 4 * CUT:4 * BW]).then_inc(sem.ld, 16)
        g.sync.dma_start(T.b_in[:, 0:4 * CUT], T.b[:, 0:4 * CUT]).then_inc(sem.lb, 16)
        g.sync.dma_start(T.a_in[:], T.a[:]).then_inc(sem.la, 16)
        g.vector.wait_ge(sem.ld, 16)
        g.vector.quantize_mx(T.bq[:, b0 + CUT:b0 + BW], T.bsc[:, b0 + CUT:b0 + BW],
                             T.b_in[:, 4 * CUT:4 * BW]).then_inc(sem.qd, 1)
        g.vector.wait_ge(sem.lb, 16)
        g.vector.quantize_mx(T.bq[:, b0:b0 + CUT], T.bsc[:, b0:b0 + CUT], T.b_in[:, 0:4 * CUT]).then_inc(sem.qb, 1)
        g.vector.wait_ge(sem.la, 16)
        g.vector.quantize_mx(T.aq[:, a0:a0 + TA * AW], T.asc[:, a0:a0 + TA * AW], T.a_in[:]).then_inc(sem.qa, 1)

    lands, calls = {}, []
    for stage, s, part, src, dst in hops:
        mask = engines(src, dst, stage >= 1 and part == ("e" if s in carried else "c"))
        if dst == core:
            lands[s, part] = (stage, (topo.chip(src) == topo.chip(core)) == (stage >= 1), _bits(mask))
        if src == core:
            if calls and calls[-1][:3] == (stage, s, part) and not any(mask & m for _, m in calls[-1][3]):
                calls[-1][3].append((dst, mask))
            else:
                calls.append((stage, s, part, [(dst, mask)]))
    a_due = rank is not None
    waited = set()
    for stage, s, part, targets in calls:
        if stage > 0 and a_due:
            a_due = False
            g.wait_ge(sem.qa, 1)
            for peer in row:
                send(lambda: T.asc[:, a0:a0 + TA * AW], [(peer, engines(core, peer))], sem.ra)
                send(lambda: T.aq[:, a0:a0 + TA * AW].bitcast(dt.uint8), [(peer, engines(core, peer))], sem.ra)
        if s != i:
            g.wait_ge(sem["b%s%d" % (part, s)], lands[s, part][2])
        else:
            for q in ("qd",) if part == "d" else ("qd", "qb") if part == "s" else ("qb",):
                if q not in waited:
                    waited.add(q)
                    g.wait_ge(sem[q], 1)
        send(piece(s, part), targets, sem["b%s%d" % (part, s)])
    g.wait_ge(sem.sent, sent[0])
    if rank is None:
        return

    def codes(s, k):
        return "d" if GROUPS[k][0] >= CUT else "e" if s in carried and GROUPS[k][0] >= MID else "c"
    todo = sorted(((s, k) for s in range(GR) for k in range(len(GROUPS))),
                  key=lambda e: (-1, 0) if e[0] == i else lands[e[0], codes(*e)][:2])
    seen, done, finish = set(), [0] * len(GROUPS), []
    for s, k in todo:
        needs = [("qa", 1) if s // TA == j else ("ra", sum(2 * _bits(engines(peer, core)) for peer in row))]
        if s == i:
            needs += [("qd", 1), ("qb", 1)]
        else:
            needs += [("b%s%d" % (part, s), lands[s, part][2]) for part in ("s", codes(s, k))]
        for name, count in needs:
            if name not in seen:
                seen.add(name)
                g.tensor.wait_ge(sem[name], count)
        done[k] += 1
        lo, hi = BW * s + GROUPS[k][0], BW * s + GROUPS[k][1]
        g.tensor.matmul_mx(T.acc[:, 512 * k:512 * k + hi - lo],
                           T.aq[:, AW * s:AW * s + AW], T.asc[:, AW * s:AW * s + AW],
                           T.bq[:, lo:hi], T.bsc[:, lo:hi],
                           done[k] == 1, done[k] == GR).then_inc(sem["mm%d" % k], 1)
        if done[k] == GR:
            finish.append(k)

    for n, k in enumerate(finish):
        lo, hi = GROUPS[k]
        mm, cp, st = sem["mm%d" % k], sem["cp%d" % k], sem["st%d" % k]
        if n % 2 == 0:
            g.vector.wait_ge(mm, GR)
            g.vector.tensor_copy(T.y_sb[:, lo:hi], T.acc[:, 512 * k:512 * k + hi - lo]).then_inc(cp, 1)
            q = g.sync
        else:
            g.scalar.wait_ge(mm, GR)
            g.scalar.activation(T.y_sb[:, lo:hi], T.acc[:, 512 * k:512 * k + hi - lo],
                                ActivationFunctionType.Copy).then_inc(cp, 1)
            q = g.scalar
        q.wait_ge(cp, 1)
        q.dma_start(T.y[:, lo:hi], T.y_sb[:, lo:hi]).then_inc(st, 16)
    for n, k in enumerate(finish):
        (g.sync if n % 2 == 0 else g.scalar).wait_ge(sem["st%d" % k], 16)
